import numpy as np
import ml_dtypes


def mxq(x, axis, fmt="e4m3"):
    dtype, down = {"e4m3": (ml_dtypes.float8_e4m3fn, 7), "e5m2": (ml_dtypes.float8_e5m2, 14)}[fmt]
    v = np.moveaxis(np.asarray(x, np.float32).astype(ml_dtypes.bfloat16).astype(np.float64), axis, -1)
    blocks = v.reshape(v.shape[:-1] + (-1, 32))
    amax = np.abs(blocks).max(-1, keepdims=True)
    byte = np.maximum(np.where(amax > 0, np.frexp(amax)[1] - 1 + 127, 0) - down, 1)
    scale = np.exp2(byte - 127.0)
    codes = (blocks / scale).astype(np.float32).astype(dtype).astype(np.float64)
    return np.moveaxis((codes * scale).reshape(v.shape), -1, axis)


WIDE = False


def mx_kscale(k):
    if not WIDE:
        return np.ones(k)
    levels = np.array([10, -10, 5, -5, 0])
    if k % 512:
        return np.exp2(np.random.permutation(np.resize(levels, k // 32))).repeat(32)
    a = np.empty((k // 512, 16))
    for p in range(k // 512):
        a[p, :8] = np.random.permutation(np.resize(levels, 8))
        for g in range(8):
            far = levels[np.abs(levels - a[p, g]) >= 10]
            a[p, g + 8] = far[np.random.randint(len(far))]
    return np.exp2(a.ravel()).repeat(32)


def f64(x):
    return np.asarray(x).astype(np.float64)


def striped(idx):
    return np.tile(idx.reshape(-1, 16).T, (8, 1)).astype(np.uint16)


def unstriped(offs):
    return offs[:16].T.reshape(-1).astype(np.int64)


E2M1 = np.array([0.0, 0.5, 1.0, 1.5, 2.0, 3.0, 4.0, 6.0, -0.0, -0.5, -1.0, -1.5, -2.0, -3.0, -4.0, -6.0])


def pack_weight(w, fmt):
    k, n = w.shape
    w = f64(np.asarray(w, np.float32).astype(ml_dtypes.bfloat16)).reshape(k // 32, 32, n)
    amax = np.abs(w).max(1)
    if fmt == "e4m3":
        byte = np.frexp(amax)[1] - 1 + 127 - 7
    else:
        mant, ex = np.frexp(amax / 6.0)
        byte = np.where(mant > 0.5, ex, ex - 1) + 127
    byte = np.clip(np.where(amax > 0, byte, 1), 1, 254)
    scaled = (w * np.exp2(127.0 - byte)[:, None, :]).reshape(k, n).astype(np.float32)
    by_word = np.ascontiguousarray(scaled.reshape(k // 512, 128, 4, n).transpose(0, 1, 3, 2))
    if fmt == "e4m3":
        words = by_word.astype(ml_dtypes.float8_e4m3fn).view(np.uint8)
    else:
        c = by_word.astype(ml_dtypes.float4_e2m1fn).view(np.uint8) & 0xF
        words = (c[..., 0::2] | (c[..., 1::2] << 4)).reshape(k // 512, 128, 2 * n)
    return np.ascontiguousarray(words), np.ascontiguousarray(byte.astype(np.uint8).reshape(k // 512, 16, n))


def unpack_weight(words, scales, fmt):
    g, _, n = scales.shape
    words = np.ascontiguousarray(words).reshape(g, 128, n, -1)
    if fmt == "e4m3":
        vals = words.view(ml_dtypes.float8_e4m3fn).astype(np.float64)
    else:
        nib = np.empty((g, 128, n, 4), np.uint8)
        nib[..., 0::2] = words & 0xF
        nib[..., 1::2] = words >> 4
        vals = E2M1[nib]
    vals = vals * np.repeat(np.exp2(scales.astype(np.float64) - 127.0), 8, axis=1)[..., None]
    return vals.transpose(0, 1, 3, 2).reshape(g * 512, n)


def gelu(v):
    return 0.5 * v * (1.0 + np.tanh(np.sqrt(2.0 / np.pi) * (v + 0.044715 * v**3)))


K, R, H, N, T, S, T2, P = 1024, 512, 1024, 384, 4096, 1024, 2048, 1024

def setup_inputs():
    n = np.random.standard_normal
    s = mx_kscale(K)[:, None]
    c = mx_kscale(R)[:, None]
    u = mx_kscale(H)[:, None]
    d = {}
    d["tab_words"], d["tab_scales"] = pack_weight(n((K, T)) * s, "e4m3")
    d["offs"] = striped(np.random.permutation(T)[:S])
    d["offs2"] = striped(np.random.permutation(T2)[:S])
    d["offs3"] = striped(np.random.permutation(T2)[:P])
    d["offs4"] = striped(np.random.permutation(T2)[:P])
    d["w1"] = (1.8 * n((K, R)) / K**0.5 / s).astype(np.float32)
    d["g1"] = (np.exp(0.3 * n(R)) * c[:, 0]).astype(np.float32)
    d["w2_words"], d["w2_scales"] = pack_weight(1.3 * n((R, H)) / R**0.5 / c, "e2m1")
    d["w3_words"], d["w3_scales"] = pack_weight(0.8 * n((K, H)) / K**0.5 / s, "e4m3")
    d["gain"] = (np.exp(0.3 * n(H)) * u[:, 0]).astype(np.float32)
    d["wgs"] = np.exp(0.3 * n((128, S))).astype(np.float32)
    d["page0"] = (1.2 * n((H, T2)) * u).astype(np.float32)
    d["wean"] = np.exp(0.4 * n(H)).astype(np.float32)
    d["w4"] = (n((H, N)) / H**0.5 / u).astype(np.float32)
    d["wgo"] = np.exp(0.3 * n((128, P))).astype(np.float32)
    d["page1"] = n((N, T2)).astype(np.float32)
    return d

def reference(tab_words, tab_scales, offs, offs2, offs3, offs4, w1, g1, w2_words, w2_scales, w3_words, w3_scales, gain, wgs, page0, wean, w4, wgo, page1):
    v = unpack_weight(tab_words, tab_scales, "e4m3")[:, unstriped(offs)]
    w2 = unpack_weight(w2_words, w2_scales, "e2m1")
    w3 = unpack_weight(w3_words, w3_scales, "e4m3")
    b = f64(g1)[:, None] * np.tanh(mxq(f64(w1), 0, "e4m3").T @ v)
    h = f64(gain)[:, None] * (w2.T @ mxq(b, 0, "e4m3") + w3.T @ v)
    page = f64(page0).copy()
    page[:, unstriped(offs2)] = np.tile(f64(wgs), (H // 128, 1)) * h
    x = f64(wean)[:, None] * page[:, unstriped(offs3)]
    y = np.abs(mxq(f64(w4), 0, "e4m3").T @ mxq(x, 0, "e4m3"))
    out = f64(page1).copy()
    out[:, unstriped(offs4)] = np.tile(f64(wgo), (N // 128, 1)) * y
    return out

@@ -1,0 +1,342 @@
+from contextlib import ExitStack
+
+import concourse.mybir as mybir
+
+K, R, H, N, T, S, T2 = 1024, 512, 1024, 384, 4096, 1024, 2048
+FLOPS = 2 * S * (K * R + R * H + K * H + H * N)
+
+F32 = mybir.dt.float32
+BF16 = mybir.dt.bfloat16
+I32 = mybir.dt.int32
+U32 = mybir.dt.uint32
+U16 = mybir.dt.uint16
+U8 = mybir.dt.uint8
+E4M3 = mybir.dt.float8_e4m3fn_x4
+E2M1 = mybir.dt.float4_e2m1fn_x4
+ACT = mybir.ActivationFunctionType
+MULT = mybir.AluOpType.mult
+
+P = 128
+PACK = 4
+HALF = 512
+UNIT = 128
+LIST_COLS = HALF // 16
+
+
+def tile_list_perfusion_console_page_kernel(
+    tc, tab_words, tab_scales, offs, offs2, offs3, offs4, w1, g1, w2_words, w2_scales,
+    w3_words, w3_scales, gain, wgs, page0, wean, w4, wgo, page1, out,
+):
+    nc = tc.nc
+
+    def half_cols(c):
+        return slice(c * HALF, (c + 1) * HALF)
+
+    def half_list(lst, c):
+        return lst[:, c * LIST_COLS : (c + 1) * LIST_COLS]
+
+    with ExitStack() as ctx:
+        keep = ctx.enter_context(tc.tile_pool(name="keep", bufs=1))
+        psum = ctx.enter_context(tc.psum_pool(name="psum", bufs=1))
+
+        def bank(i, shape):
+            return psum.tile(shape, F32, name=f"bank{i}")
+
+        idx = keep.tile([P, S // 16], U16)
+        idx2 = keep.tile([P, S // 16], U16)
+        idx3 = keep.tile([P, S // 16], U16)
+        idx4 = keep.tile([P, S // 16], U16)
+        g1_sb = keep.tile([P, PACK], F32)
+        gain_sb = keep.tile([P, 2, PACK], F32)
+        wean_sb = keep.tile([P, 2, PACK], F32)
+        v_codes = [[keep.tile([P, HALF], U32, name=f"v_codes{a}{c}", align_bytes=64) for c in range(2)] for a in range(2)]
+        v_scales = keep.tile([P, S], U8, align_bytes=64)
+        w1_codes = [keep.tile([P, R], U32, name=f"w1_codes{a}", align_bytes=64) for a in range(2)]
+        w1_scales = [keep.tile([P, R], U8, name=f"w1_scales{a}", align_bytes=64) for a in range(2)]
+        w3_codes = [keep.tile([P, 2, HALF], I32, name=f"w3_codes{b}", align_bytes=64) for b in range(2)]
+        w2_codes = [keep.tile([P, 2 * HALF], U8, name=f"w2_codes{b}", align_bytes=64) for b in range(2)]
+        w23_scales = [keep.tile([P, HALF], U8, name=f"w23_scales{b}", align_bytes=64) for b in range(2)]
+        b_codes = [keep.tile([P, HALF], U32, name="b_codes0", align_bytes=64)]
+        b_scales = [keep.tile([P, HALF], U8, name=f"b_scales{c}", align_bytes=64) for c in range(2)]
+        wgs_sb = [keep.tile([P, PACK, HALF], F32, name=f"wgs_sb{c}", align_bytes=64) for c in range(2)]
+        pages = [keep.tile([P, T2], F32, name=f"page{i}") for i in range(8)]
+
+        def load_wgs(c, quad):
+            rows = wgs.rearrange("(q t) s -> q t s", t=PACK)[:, :, half_cols(c)]
+            nc.sync.dma_start(out=wgs_sb[c][32 * quad : 32 * quad + 32, :, :], in_=rows)
+
+        def new_states(i, c, acc):
+            blk, t = divmod(i, PACK)
+            cols = slice(t * P, (t + 1) * P)
+            for a in range(2):
+                nc.tensor.matmul_mx(
+                    out=acc[:], lhsT=w3_codes[blk][:, a, cols].bitcast(E4M3),
+                    lhsT_scale=w23_scales[blk][4 + 4 * a : P, cols],
+                    rhs=v_codes[a][c][:].bitcast(E4M3), rhs_scale=v_scales[4 * a : P, half_cols(c)],
+                    start=(a == 0), stop=False,
+                )
+            nc.tensor.matmul_mx(
+                out=acc[:], lhsT=w2_codes[blk][:, 2 * t * P : 2 * (t + 1) * P].bitcast(E2M1),
+                lhsT_scale=w23_scales[blk][:, cols],
+                rhs=b_codes[c][:].bitcast(E4M3), rhs_scale=b_scales[c][:],
+                start=False, stop=True,
+            )
+            h = keep.tile([P, HALF], F32, name="h_spare" if (i, c) == (4, 1) else f"h{i}", align_bytes=64)
+            nc.scalar.activation(out=h[:], in_=acc[:], func=ACT.Copy, scale=gain_sb[:, blk, t : t + 1])
+            nc.vector.tensor_tensor(
+                out=pages[i][:].indirect(half_list(idx2, c)), in0=h[:], in1=wgs_sb[c][:, t, :], op=MULT
+            )
+
+        with tc.tile_pool(name="head", bufs=1) as head:
+            tab_sb = [head.tile([P, T], I32, name=f"tab_sb{a}") for a in range(2)]
+            tab_scales_sb = head.tile([P, T], U8)
+            w1_raw = [head.tile([P, PACK, R], F32, name=f"w1_raw{a}") for a in range(2)]
+            w3_raw = [head.tile([P, 2, HALF], I32, name=f"w3_raw{b}") for b in range(2)]
+            w2_raw = [head.tile([P, 2 * HALF], U8, name=f"w2_raw{b}") for b in range(2)]
+            w23_scales_raw = head.tile([P, H], U8)
+
+            nc.vector.memset(tab_scales_sb[:].bitcast(I32), 0)
+            nc.gpsimd.memset(w23_scales_raw[:].bitcast(I32), 0)
+            for quad in range(4):
+                nc.scalar.dma_start(
+                    out=tab_scales_sb[32 * quad : 32 * quad + 8, :].bitcast(I32),
+                    in_=tab_scales[:, 4 * quad : 4 * quad + 4, :].bitcast(I32),
+                )
+            nc.gpsimd.dma_start(out=g1_sb[:], in_=g1.rearrange("(p t) -> p t", t=PACK))
+            for quad in range(4):
+                nc.gpsimd.dma_start(
+                    out=w23_scales_raw[32 * quad + 4 : 32 * quad + 12, :].bitcast(I32),
+                    in_=w3_scales[:, 4 * quad : 4 * quad + 4, :].bitcast(I32),
+                )
+            nc.gpsimd.dma_start(out=gain_sb[:], in_=gain.rearrange("(b p t) -> p b t", b=2, t=PACK))
+            nc.gpsimd.dma_start(out=wean_sb[:], in_=wean.rearrange("(b p t) -> p b t", b=2, t=PACK))
+
+            def load_w23(blk):
+                w3_bytes = w3_words.rearrange("a p n i -> p a (n i)")
+                nc.sync.dma_start(
+                    out=w3_raw[blk][:], in_=w3_bytes[:, :, 4 * HALF * blk : 4 * HALF * (blk + 1)].bitcast(I32)
+                )
+                nc.sync.dma_start(
+                    out=w2_raw[blk][:].bitcast(I32),
+                    in_=w2_words[0, :, 2 * HALF * blk : 2 * HALF * (blk + 1)].bitcast(I32),
+                )
+
+            def load_w1(a):
+                nc.sync.dma_start(
+                    out=w1_raw[a][:], in_=w1[512 * a : 512 * (a + 1), :].rearrange("(p j) m -> p j m", j=PACK)
+                )
+
+            def load_tab(a):
+                nc.sync.dma_start(out=tab_sb[a][:], in_=tab_words[a].rearrange("p t i -> p (t i)").bitcast(I32))
+
+            def load_w2_scales(quad):
+                nc.sync.dma_start(
+                    out=w23_scales_raw[32 * quad : 32 * quad + 4, :].bitcast(I32),
+                    in_=w2_scales[0, 4 * quad : 4 * quad + 4, :].bitcast(I32),
+                )
+
+            def load_page(i):
+                rows = page0.rearrange("(b p t) c -> b t p c", b=2, t=PACK)
+                nc.sync.dma_start(out=pages[i][:], in_=rows[i // PACK, i % PACK])
+
+            nc.sync.dma_start(idx[:], offs)
+            load_tab(0)
+            load_w1(0)
+            load_w1(1)
+            load_w23(0)
+            load_tab(1)
+            load_wgs(0, 0)
+            load_wgs(0, 1)
+            for quad in (0, 2):
+                load_w2_scales(quad)
+                load_w2_scales(quad + 1)
+                load_wgs(0, 2 + quad // 2)
+            nc.sync.dma_start(idx2[:], offs2)
+            load_page(0)
+            load_w23(1)
+            for i in range(1, 8):
+                load_page(i)
+            for quad in range(4):
+                load_wgs(1, quad)
+            nc.sync.dma_start(idx3[:], offs3)
+            nc.sync.dma_start(idx4[:], offs4)
+
+            def deal_w23(blk):
+                nc.vector.tensor_copy(
+                    out=w3_codes[blk][:].rearrange("p a (t c i) -> p a c t i", t=PACK, i=4),
+                    in_=w3_raw[blk][:].rearrange("p a (c i t) -> p a c t i", t=PACK, i=4),
+                )
+                nc.vector.tensor_copy(
+                    out=w2_codes[blk][:].bitcast(U16).rearrange("p (t c i) -> p c t i", t=PACK, i=8),
+                    in_=w2_raw[blk][:].bitcast(U16).rearrange("p (c i t) -> p c t i", t=PACK, i=8),
+                )
+                nc.vector.tensor_copy(
+                    out=w23_scales[blk][:].rearrange("p (t c i) -> p c t i", t=PACK, i=16),
+                    in_=w23_scales_raw[:, half_cols(blk)].rearrange("p (c i t) -> p c t i", t=PACK, i=16),
+                )
+
+            def quantise_w1(a):
+                grouped = head.tile([P, PACK * R], BF16, name=f"w1_grouped{a}", align_bytes=64)
+                nc.scalar.copy(
+                    out=grouped[:].rearrange("p (t m j) -> p m t j", t=PACK, j=PACK),
+                    in_=w1_raw[a][:].rearrange("p j (m t) -> p m t j", t=PACK),
+                )
+                nc.vector.quantize_mx(out=w1_codes[a][:].bitcast(E4M3), scales=w1_scales[a][:], in_=grouped[:])
+
+            def gather_words(a, c):
+                nc.vector.tensor_copy(
+                    out=v_codes[a][c][:], in_=tab_sb[a][:].bitcast(U32).indirect(half_list(idx, c))
+                )
+
+            def features(acc, t, a, c, cols, start, stop):
+                nc.tensor.matmul_mx(
+                    out=acc, lhsT=w1_codes[a][:, t * P : (t + 1) * P].bitcast(E4M3),
+                    lhsT_scale=w1_scales[a][:, t * P : (t + 1) * P],
+                    rhs=v_codes[a][c][:, cols].bitcast(E4M3),
+                    rhs_scale=v_scales[4 * a : P, c * HALF + cols.start : c * HALF + cols.stop],
+                    start=start, stop=stop,
+                )
+
+            gather_words(0, 0)
+            gather_words(0, 1)
+            nc.vector.tensor_copy(out=v_scales[:], in_=tab_scales_sb[:].indirect(idx[:]))
+            quantise_w1(0)
+            quantise_w1(1)
+            deal_w23(0)
+            unit_cols = [slice(u * UNIT, (u + 1) * UNIT) for u in range(HALF // UNIT)]
+            unit_acc = [bank(u, [P, PACK, UNIT]) for u in range(HALF // UNIT)]
+            for u, cols in enumerate(unit_cols):
+                for t in range(PACK):
+                    features(unit_acc[u][:, t, :], t, 0, 0, cols, t == 0, False)
+            gather_words(1, 0)
+
+            b_grouped = [head.tile([P, HALF, PACK], BF16, name=f"b_grouped{c}", align_bytes=64) for c in range(2)]
+            for u, cols in enumerate(unit_cols):
+                for t in range(PACK):
+                    features(unit_acc[u][:, t, :], t, 1, 0, cols, False, t == PACK - 1)
+                bounded = head.tile([P, UNIT, PACK], F32, name=f"bounded_unit{u}")
+                nc.scalar.activation(out=bounded[:], in_=unit_acc[u][:].rearrange("p t n -> p n t"), func=ACT.Tanh)
+                nc.vector.tensor_tensor(
+                    out=b_grouped[0][:, cols, :], in0=bounded[:],
+                    in1=g1_sb[:].unsqueeze(1).to_broadcast([P, UNIT, PACK]), op=MULT,
+                )
+                if u % 2 == 1:
+                    pair = slice((u - 1) * UNIT, (u + 1) * UNIT)
+                    nc.vector.quantize_mx(
+                        out=b_codes[0][:, pair].bitcast(E4M3), scales=b_scales[0][:, pair],
+                        in_=b_grouped[0][:, pair, :].rearrange("p n t -> p (n t)"),
+                    )
+            gather_words(1, 1)
+
+            for i in range(8):
+                if i == 1:
+                    deal_w23(1)
+                new_states(i, 0, bank(4 + i if i < 2 else 6 + i % 2, [P, HALF]))
+
+            for t in range(PACK):
+                acc = bank(4 + t % 2, [P, HALF])
+                for a in range(2):
+                    features(acc[:], t, a, 1, slice(0, HALF), a == 0, a == 1)
+                bounded = head.tile([P, HALF], F32, name="bounded", bufs=2)
+                nc.scalar.activation(out=bounded[:], in_=acc[:], func=ACT.Tanh)
+                nc.scalar.activation(
+                    out=b_grouped[1][:, :, t], in_=bounded[:], func=ACT.Copy, scale=g1_sb[:, t : t + 1]
+                )
+            b_codes.append(keep.tile([P, HALF], U32, name="h4", align_bytes=64))
+            nc.vector.quantize_mx(
+                out=b_codes[1][:].bitcast(E4M3), scales=b_scales[1][:],
+                in_=b_grouped[1][:].rearrange("p n t -> p (n t)"),
+            )
+
+        tail = ctx.enter_context(tc.tile_pool(name="tail", bufs=1))
+        n_tiles = N // P
+        w4_raw = tail.tile([P, 2, PACK, N], F32)
+        w4_grouped = tail.tile([P, n_tiles, 2, P, PACK], BF16, align_bytes=64)
+        w4_scales = tail.tile([P, n_tiles, 2 * P], U8, align_bytes=64)
+        wgo_sb = tail.tile([P, S], F32)
+        pumps = [tail.tile([P, T2], F32, name=f"pump{n}") for n in range(n_tiles)]
+        x_grouped = [[tail.tile([P, HALF, PACK], BF16, name=f"x_grouped{b}{c}", align_bytes=64) for c in range(2)] for b in range(2)]
+        x_scales = [[tail.tile([P, HALF], U8, name=f"x_scales{b}{c}", align_bytes=64) for c in range(2)] for b in range(2)]
+        y_acc = [[bank(3 * c + n, [P, HALF]) for n in range(n_tiles)] for c in range(2)]
+
+        nc.sync.dma_start(out=w4_raw[:], in_=w4.rearrange("(b p j) n -> p b j n", b=2, j=PACK))
+        nc.sync.dma_start(out=wgo_sb[:], in_=wgo)
+        for n in range(n_tiles):
+            nc.sync.dma_start(out=pumps[n][:], in_=page1[n * P : (n + 1) * P, :])
+
+        for n in range(n_tiles):
+            for blk in range(2):
+                nc.scalar.copy(
+                    out=w4_grouped[:, n, blk].rearrange("p (c i) j -> p c j i", i=4),
+                    in_=w4_raw[:, blk, :, n * P : (n + 1) * P].rearrange("p j (c i) -> p c j i", i=4),
+                )
+
+        def recall(i, c):
+            blk, t = divmod(i, PACK)
+            picked = tail.tile([P, HALF], F32, name="picked", bufs=8)
+            nc.vector.tensor_copy(out=picked[:], in_=pages[i][:].indirect(half_list(idx3, c)))
+            nc.scalar.activation(
+                out=x_grouped[blk][c][:, :, t], in_=picked[:], func=ACT.Copy, scale=wean_sb[:, blk, t : t + 1]
+            )
+
+        new_states(0, 1, bank(6, [P, HALF]))
+        for i in range(1, 8):
+            new_states(i, 1, bank(6 + i % 2, [P, HALF]))
+            recall(i - 1, 0)
+            recall(i - 1, 1)
+        recall(7, 0)
+        recall(7, 1)
+
+        late_codes = keep.tile([P, 2 * N + 2 * HALF], U32, name="wgs_sb1", align_bytes=64)
+        w4_codes = [late_codes[:, 2 * P * n : 2 * P * (n + 1)] for n in range(n_tiles)]
+        x_codes = [
+            [late_codes[:, 2 * N + c * HALF : 2 * N + (c + 1) * HALF] for c in range(2)],
+            [tail.tile([P, HALF], U32, name=f"x_codes1{c}", align_bytes=64)[:] for c in range(2)],
+        ]
+
+        def quantise_w4(n):
+            nc.vector.quantize_mx(
+                out=w4_codes[n].bitcast(E4M3), scales=w4_scales[:, n, :],
+                in_=w4_grouped[:, n].rearrange("p b m j -> p (b m j)"),
+            )
+
+        def quantise_x(blk, c):
+            nc.vector.quantize_mx(
+                out=x_codes[blk][c].bitcast(E4M3), scales=x_scales[blk][c][:],
+                in_=x_grouped[blk][c][:].rearrange("p n t -> p (n t)"),
+            )
+
+        def pump_pass(n, blk, c):
+            cols = slice(blk * P, (blk + 1) * P)
+            nc.tensor.matmul_mx(
+                out=y_acc[c][n][:], lhsT=w4_codes[n][:, cols].bitcast(E4M3), lhsT_scale=w4_scales[:, n, cols],
+                rhs=x_codes[blk][c].bitcast(E4M3), rhs_scale=x_scales[blk][c][:],
+                start=(blk == 0), stop=(blk == 1),
+            )
+
+        def place(n, c):
+            y = tail.tile([P, HALF], F32, name=f"y{n}{c}")
+            nc.scalar.activation(out=y[:], in_=y_acc[c][n][:], func=ACT.Abs)
+            nc.vector.tensor_tensor(
+                out=pumps[n][:].indirect(half_list(idx4, c)), in0=y[:], in1=wgo_sb[:, half_cols(c)], op=MULT
+            )
+
+        quantise_w4(0)
+        quantise_x(0, 0)
+        pump_pass(0, 0, 0)
+        quantise_x(1, 0)
+        pump_pass(0, 1, 0)
+        for n in range(1, n_tiles):
+            quantise_w4(n)
+        quantise_x(0, 1)
+        quantise_x(1, 1)
+        place(0, 0)
+        for n in range(1, n_tiles):
+            for blk in range(2):
+                pump_pass(n, blk, 0)
+            place(n, 0)
+        for n in range(n_tiles):
+            for blk in range(2):
+                pump_pass(n, blk, 1)
+            place(n, 1)
+            nc.sync.dma_start(out=out[n * P : (n + 1) * P, :], in_=pumps[n][:])

@@ -49,21 +49,22 @@ def tile_list_perfusion_console_page_kernel(
         g1_sb = keep.tile([P, PACK], F32)
         gain_sb = keep.tile([P, 2, PACK], F32)
         wean_sb = keep.tile([P, 2, PACK], F32)
-        v_codes = [[keep.tile([P, HALF], U32, name=f"v_codes{a}{c}", align_bytes=64) for c in range(2)] for a in range(2)]
+        v_codes = {}
         v_scales = keep.tile([P, S], U8, align_bytes=64)
         w1_codes = [keep.tile([P, R], U32, name=f"w1_codes{a}", align_bytes=64) for a in range(2)]
         w1_scales = [keep.tile([P, R], U8, name=f"w1_scales{a}", align_bytes=64) for a in range(2)]
         w3_codes = [keep.tile([P, 2, HALF], I32, name=f"w3_codes{b}", align_bytes=64) for b in range(2)]
-        w2_codes = [keep.tile([P, 2 * HALF], U8, name=f"w2_codes{b}", align_bytes=64) for b in range(2)]
-        w23_scales = [keep.tile([P, HALF], U8, name=f"w23_scales{b}", align_bytes=64) for b in range(2)]
+        w2_codes = keep.tile([P, 2 * H], U8, align_bytes=64)
+        w23_scales = keep.tile([P, H], U8, align_bytes=64)
         b_codes = [keep.tile([P, HALF], U32, name="b_codes0", align_bytes=64)]
         b_scales = [keep.tile([P, HALF], U8, name=f"b_scales{c}", align_bytes=64) for c in range(2)]
         wgs_sb = [keep.tile([P, PACK, HALF], F32, name=f"wgs_sb{c}", align_bytes=64) for c in range(2)]
         pages = [keep.tile([P, T2], F32, name=f"page{i}") for i in range(8)]
 
-        def load_wgs(c, quad):
-            rows = wgs.rearrange("(q t) s -> q t s", t=PACK)[:, :, half_cols(c)]
-            nc.sync.dma_start(out=wgs_sb[c][32 * quad : 32 * quad + 32, :, :], in_=rows)
+        def load_wgs(c, slots):
+            rows = wgs.rearrange("(q t) s -> q t s", t=PACK)[:, slots, half_cols(c)]
+            for quad in (0, 2, 1, 3):
+                nc.sync.dma_start(out=wgs_sb[c][32 * quad : 32 * quad + 32, slots, :], in_=rows)
 
         def new_states(i, c, acc):
             blk, t = divmod(i, PACK)
@@ -71,13 +72,13 @@ def tile_list_perfusion_console_page_kernel(
             for a in range(2):
                 nc.tensor.matmul_mx(
                     out=acc[:], lhsT=w3_codes[blk][:, a, cols].bitcast(E4M3),
-                    lhsT_scale=w23_scales[blk][4 + 4 * a : P, cols],
-                    rhs=v_codes[a][c][:].bitcast(E4M3), rhs_scale=v_scales[4 * a : P, half_cols(c)],
+                    lhsT_scale=w23_scales[4 + 4 * a : P, i * P : (i + 1) * P],
+                    rhs=v_codes[a, c][:].bitcast(E4M3), rhs_scale=v_scales[4 * a : P, half_cols(c)],
                     start=(a == 0), stop=False,
                 )
             nc.tensor.matmul_mx(
-                out=acc[:], lhsT=w2_codes[blk][:, 2 * t * P : 2 * (t + 1) * P].bitcast(E2M1),
-                lhsT_scale=w23_scales[blk][:, cols],
+                out=acc[:], lhsT=w2_codes[:, 2 * i * P : 2 * (i + 1) * P].bitcast(E2M1),
+                lhsT_scale=w23_scales[:, i * P : (i + 1) * P],
                 rhs=b_codes[c][:].bitcast(E4M3), rhs_scale=b_scales[c][:],
                 start=False, stop=True,
             )
@@ -92,33 +93,26 @@ def tile_list_perfusion_console_page_kernel(
             tab_scales_sb = head.tile([P, T], U8)
             w1_raw = [head.tile([P, PACK, R], F32, name=f"w1_raw{a}") for a in range(2)]
             w3_raw = [head.tile([P, 2, HALF], I32, name=f"w3_raw{b}") for b in range(2)]
-            w2_raw = [head.tile([P, 2 * HALF], U8, name=f"w2_raw{b}") for b in range(2)]
+            w2_raw = head.tile([P, 2 * H], U8)
             w23_scales_raw = head.tile([P, H], U8)
 
-            nc.vector.memset(tab_scales_sb[:].bitcast(I32), 0)
+            nc.gpsimd.memset(tab_scales_sb[:].bitcast(I32), 0)
             nc.gpsimd.memset(w23_scales_raw[:].bitcast(I32), 0)
             for quad in range(4):
-                nc.scalar.dma_start(
+                nc.gpsimd.dma_start(
                     out=tab_scales_sb[32 * quad : 32 * quad + 8, :].bitcast(I32),
                     in_=tab_scales[:, 4 * quad : 4 * quad + 4, :].bitcast(I32),
                 )
-            nc.gpsimd.dma_start(out=g1_sb[:], in_=g1.rearrange("(p t) -> p t", t=PACK))
             for quad in range(4):
                 nc.gpsimd.dma_start(
                     out=w23_scales_raw[32 * quad + 4 : 32 * quad + 12, :].bitcast(I32),
                     in_=w3_scales[:, 4 * quad : 4 * quad + 4, :].bitcast(I32),
                 )
-            nc.gpsimd.dma_start(out=gain_sb[:], in_=gain.rearrange("(b p t) -> p b t", b=2, t=PACK))
-            nc.gpsimd.dma_start(out=wean_sb[:], in_=wean.rearrange("(b p t) -> p b t", b=2, t=PACK))
 
-            def load_w23(blk):
+            def load_w3(blk):
                 w3_bytes = w3_words.rearrange("a p n i -> p a (n i)")
                 nc.sync.dma_start(
                     out=w3_raw[blk][:], in_=w3_bytes[:, :, 4 * HALF * blk : 4 * HALF * (blk + 1)].bitcast(I32)
-                )
-                nc.sync.dma_start(
-                    out=w2_raw[blk][:].bitcast(I32),
-                    in_=w2_words[0, :, 2 * HALF * blk : 2 * HALF * (blk + 1)].bitcast(I32),
                 )
 
             def load_w1(a):
@@ -129,50 +123,47 @@ def tile_list_perfusion_console_page_kernel(
             def load_tab(a):
                 nc.sync.dma_start(out=tab_sb[a][:], in_=tab_words[a].rearrange("p t i -> p (t i)").bitcast(I32))
 
+            def load_page(i):
+                rows = page0.rearrange("(b p t) c -> b t p c", b=2, t=PACK)
+                nc.sync.dma_start(out=pages[i][:], in_=rows[i // PACK, i % PACK])
+
             def load_w2_scales(quad):
                 nc.sync.dma_start(
                     out=w23_scales_raw[32 * quad : 32 * quad + 4, :].bitcast(I32),
                     in_=w2_scales[0, 4 * quad : 4 * quad + 4, :].bitcast(I32),
                 )
 
-            def load_page(i):
-                rows = page0.rearrange("(b p t) c -> b t p c", b=2, t=PACK)
-                nc.sync.dma_start(out=pages[i][:], in_=rows[i // PACK, i % PACK])
-
             nc.sync.dma_start(idx[:], offs)
             load_tab(0)
             load_w1(0)
-            load_w1(1)
-            load_w23(0)
-            load_tab(1)
-            load_wgs(0, 0)
-            load_wgs(0, 1)
-            for quad in (0, 2):
-                load_w2_scales(quad)
-                load_w2_scales(quad + 1)
-                load_wgs(0, 2 + quad // 2)
+            nc.sync.dma_start(out=g1_sb[:], in_=g1.rearrange("(p t) -> p t", t=PACK))
+            nc.sync.dma_start(out=gain_sb[:], in_=gain.rearrange("(b p t) -> p b t", b=2, t=PACK))
             nc.sync.dma_start(idx2[:], offs2)
-            load_page(0)
-            load_w23(1)
-            for i in range(1, 8):
-                load_page(i)
-            for quad in range(4):
-                load_wgs(1, quad)
             nc.sync.dma_start(idx3[:], offs3)
             nc.sync.dma_start(idx4[:], offs4)
+            load_w1(1)
+            nc.sync.dma_start(out=w2_raw[:].bitcast(I32), in_=w2_words[0].bitcast(I32))
+            load_tab(1)
+            load_w3(0)
+            for quad in range(4):
+                load_w2_scales(quad)
+            load_wgs(0, slice(0, 2))
+            load_page(0)
+            load_w3(1)
+            load_page(1)
+            load_wgs(0, slice(2, 4))
+            for i in range(2, 8):
+                load_page(i)
+            load_wgs(1, slice(0, 4))
+            nc.sync.dma_start(out=wean_sb[:], in_=wean.rearrange("(b p t) -> p b t", b=2, t=PACK))
 
-            def deal_w23(blk):
+            warm = head.tile([P, 1], F32)
+            nc.scalar.activation(out=warm[:], in_=g1_sb[:, 0:1], func=ACT.Tanh)
+
+            def deal_w3(blk):
                 nc.vector.tensor_copy(
                     out=w3_codes[blk][:].rearrange("p a (t c i) -> p a c t i", t=PACK, i=4),
                     in_=w3_raw[blk][:].rearrange("p a (c i t) -> p a c t i", t=PACK, i=4),
-                )
-                nc.vector.tensor_copy(
-                    out=w2_codes[blk][:].bitcast(U16).rearrange("p (t c i) -> p c t i", t=PACK, i=8),
-                    in_=w2_raw[blk][:].bitcast(U16).rearrange("p (c i t) -> p c t i", t=PACK, i=8),
-                )
-                nc.vector.tensor_copy(
-                    out=w23_scales[blk][:].rearrange("p (t c i) -> p c t i", t=PACK, i=16),
-                    in_=w23_scales_raw[:, half_cols(blk)].rearrange("p (c i t) -> p c t i", t=PACK, i=16),
                 )
 
             def quantise_w1(a):
@@ -183,34 +174,43 @@ def tile_list_perfusion_console_page_kernel(
                 )
                 nc.vector.quantize_mx(out=w1_codes[a][:].bitcast(E4M3), scales=w1_scales[a][:], in_=grouped[:])
 
-            def gather_words(a, c):
+            def gather_words(a, c, name):
+                v_codes[a, c] = keep.tile([P, HALF], U32, name=name, align_bytes=64)
                 nc.vector.tensor_copy(
-                    out=v_codes[a][c][:], in_=tab_sb[a][:].bitcast(U32).indirect(half_list(idx, c))
+                    out=v_codes[a, c][:], in_=tab_sb[a][:].bitcast(U32).indirect(half_list(idx, c))
                 )
 
             def features(acc, t, a, c, cols, start, stop):
                 nc.tensor.matmul_mx(
                     out=acc, lhsT=w1_codes[a][:, t * P : (t + 1) * P].bitcast(E4M3),
                     lhsT_scale=w1_scales[a][:, t * P : (t + 1) * P],
-                    rhs=v_codes[a][c][:, cols].bitcast(E4M3),
+                    rhs=v_codes[a, c][:, cols].bitcast(E4M3),
                     rhs_scale=v_scales[4 * a : P, c * HALF + cols.start : c * HALF + cols.stop],
                     start=start, stop=stop,
                 )
 
-            gather_words(0, 0)
-            gather_words(0, 1)
+            gather_words(0, 0, "v_codes00")
+            gather_words(0, 1, "v_codes01")
             nc.vector.tensor_copy(out=v_scales[:], in_=tab_scales_sb[:].indirect(idx[:]))
             quantise_w1(0)
             quantise_w1(1)
-            deal_w23(0)
+            nc.vector.tensor_copy(
+                out=w2_codes[:].bitcast(U16).rearrange("p (b t c i) -> p b c t i", b=2, t=PACK, i=8),
+                in_=w2_raw[:].bitcast(U16).rearrange("p (b c i t) -> p b c t i", b=2, t=PACK, i=8),
+            )
             unit_cols = [slice(u * UNIT, (u + 1) * UNIT) for u in range(HALF // UNIT)]
             unit_acc = [bank(u, [P, PACK, UNIT]) for u in range(HALF // UNIT)]
             for u, cols in enumerate(unit_cols):
                 for t in range(PACK):
                     features(unit_acc[u][:, t, :], t, 0, 0, cols, t == 0, False)
-            gather_words(1, 0)
+            gather_words(1, 0, "v_codes10")
+            deal_w3(0)
+            nc.vector.tensor_copy(
+                out=w23_scales[:].rearrange("p (b t c i) -> p b c t i", b=2, t=PACK, i=16),
+                in_=w23_scales_raw[:].rearrange("p (b c i t) -> p b c t i", b=2, t=PACK, i=16),
+            )
 
-            b_grouped = [head.tile([P, HALF, PACK], BF16, name=f"b_grouped{c}", align_bytes=64) for c in range(2)]
+            b_grouped = [pool.tile([P, HALF, PACK], BF16, name=f"b_grouped{c}", align_bytes=64) for c, pool in enumerate((keep, head))]
             for u, cols in enumerate(unit_cols):
                 for t in range(PACK):
                     features(unit_acc[u][:, t, :], t, 1, 0, cols, False, t == PACK - 1)
@@ -226,11 +226,11 @@ def tile_list_perfusion_console_page_kernel(
                         out=b_codes[0][:, pair].bitcast(E4M3), scales=b_scales[0][:, pair],
                         in_=b_grouped[0][:, pair, :].rearrange("p n t -> p (n t)"),
                     )
-            gather_words(1, 1)
+            gather_words(1, 1, "b_grouped0")
 
             for i in range(8):
                 if i == 1:
-                    deal_w23(1)
+                    deal_w3(1)
                 new_states(i, 0, bank(4 + i if i < 2 else 6 + i % 2, [P, HALF]))
 
             for t in range(PACK):
@@ -271,21 +271,24 @@ def tile_list_perfusion_console_page_kernel(
                     in_=w4_raw[:, blk, :, n * P : (n + 1) * P].rearrange("p j (c i) -> p c j i", i=4),
                 )
 
-        def recall(i, c):
+        def recall(i, halves):
             blk, t = divmod(i, PACK)
-            picked = tail.tile([P, HALF], F32, name="picked", bufs=8)
-            nc.vector.tensor_copy(out=picked[:], in_=pages[i][:].indirect(half_list(idx3, c)))
-            nc.scalar.activation(
-                out=x_grouped[blk][c][:, :, t], in_=picked[:], func=ACT.Copy, scale=wean_sb[:, blk, t : t + 1]
-            )
+            picked = tail.tile([P, len(halves), HALF], F32, name="picked", bufs=4)
+            entries = idx3[:, halves[0] * LIST_COLS : (halves[-1] + 1) * LIST_COLS]
+            nc.vector.tensor_copy(out=picked[:].rearrange("p c n -> p (c n)"), in_=pages[i][:].indirect(entries))
+            for k, c in enumerate(halves):
+                nc.scalar.activation(
+                    out=x_grouped[blk][c][:, :, t], in_=picked[:, k, :], func=ACT.Copy, scale=wean_sb[:, blk, t : t + 1]
+                )
 
         new_states(0, 1, bank(6, [P, HALF]))
         for i in range(1, 8):
             new_states(i, 1, bank(6 + i % 2, [P, HALF]))
-            recall(i - 1, 0)
-            recall(i - 1, 1)
-        recall(7, 0)
-        recall(7, 1)
+            if i < 7:
+                recall(i - 1, (0, 1))
+        for c in range(2):
+            recall(6, (c,))
+            recall(7, (c,))
 
         late_codes = keep.tile([P, 2 * N + 2 * HALF], U32, name="wgs_sb1", align_bytes=64)
         w4_codes = [late_codes[:, 2 * P * n : 2 * P * (n + 1)] for n in range(n_tiles)]

@@ -18,9 +18,12 @@ MULT = mybir.AluOpType.mult
 
 P = 128
 PACK = 4
+PASS = P * PACK
 HALF = 512
 UNIT = 128
 LIST_COLS = HALF // 16
+ROW_TILES = H // P
+B_LATE_TILE = 4
 
 
 def tile_list_perfusion_console_page_kernel(
@@ -53,46 +56,54 @@ def tile_list_perfusion_console_page_kernel(
         v_scales = keep.tile([P, S], U8, align_bytes=64)
         w1_codes = [keep.tile([P, R], U32, name=f"w1_codes{a}", align_bytes=64) for a in range(2)]
         w1_scales = [keep.tile([P, R], U8, name=f"w1_scales{a}", align_bytes=64) for a in range(2)]
-        w3_codes = [keep.tile([P, 2, HALF], I32, name=f"w3_codes{b}", align_bytes=64) for b in range(2)]
+        w3_codes = [keep.tile([P, 2, PASS], I32, name=f"w3_codes{b}", align_bytes=64) for b in range(2)]
         w2_codes = keep.tile([P, 2 * H], U8, align_bytes=64)
         w23_scales = keep.tile([P, H], U8, align_bytes=64)
         b_codes = [keep.tile([P, HALF], U32, name="b_codes0", align_bytes=64)]
         b_scales = [keep.tile([P, HALF], U8, name=f"b_scales{c}", align_bytes=64) for c in range(2)]
         wgs_sb = [keep.tile([P, PACK, HALF], F32, name=f"wgs_sb{c}", align_bytes=64) for c in range(2)]
-        pages = [keep.tile([P, T2], F32, name=f"page{i}") for i in range(8)]
+        pages = [keep.tile([P, T2], F32, name=f"page{i}") for i in range(ROW_TILES)]
 
         def load_wgs(c, slots):
             rows = wgs.rearrange("(q t) s -> q t s", t=PACK)[:, slots, half_cols(c)]
             for quad in (0, 2, 1, 3):
                 nc.sync.dma_start(out=wgs_sb[c][32 * quad : 32 * quad + 32, slots, :], in_=rows)
 
-        def new_states(i, c, acc):
+        def new_states(i, c, acc, cols, h_name):
             blk, t = divmod(i, PACK)
-            cols = slice(t * P, (t + 1) * P)
+            dealt = slice(i * P, (i + 1) * P)
+            width = cols.stop - cols.start
+            entries = slice(c * HALF + cols.start, c * HALF + cols.stop)
             for a in range(2):
                 nc.tensor.matmul_mx(
-                    out=acc[:], lhsT=w3_codes[blk][:, a, cols].bitcast(E4M3),
-                    lhsT_scale=w23_scales[4 + 4 * a : P, i * P : (i + 1) * P],
-                    rhs=v_codes[a, c][:].bitcast(E4M3), rhs_scale=v_scales[4 * a : P, half_cols(c)],
+                    out=acc[:], lhsT=w3_codes[blk][:, a, t * P : (t + 1) * P].bitcast(E4M3),
+                    lhsT_scale=w23_scales[4 + 4 * a : P, dealt],
+                    rhs=v_codes[a, c][:, cols].bitcast(E4M3), rhs_scale=v_scales[4 * a : P, entries],
                     start=(a == 0), stop=False,
                 )
-            nc.tensor.matmul_mx(
-                out=acc[:], lhsT=w2_codes[:, 2 * i * P : 2 * (i + 1) * P].bitcast(E2M1),
-                lhsT_scale=w23_scales[:, i * P : (i + 1) * P],
-                rhs=b_codes[c][:].bitcast(E4M3), rhs_scale=b_scales[c][:],
-                start=False, stop=True,
-            )
-            h = keep.tile([P, HALF], F32, name="h_spare" if (i, c) == (4, 1) else f"h{i}", align_bytes=64)
+            step = HALF if width == HALF else UNIT
+            for lo in range(0, width, step):
+                part = slice(cols.start + lo, cols.start + lo + step)
+                nc.tensor.matmul_mx(
+                    out=acc[:, lo : lo + step], lhsT=w2_codes[:, 2 * i * P : 2 * (i + 1) * P].bitcast(E2M1),
+                    lhsT_scale=w23_scales[:, dealt],
+                    rhs=b_codes[c][:, part].bitcast(E4M3), rhs_scale=b_scales[c][:, part],
+                    start=False, stop=(lo + step == width),
+                )
+            h = keep.tile([P, width], F32, name=h_name, align_bytes=64)
             nc.scalar.activation(out=h[:], in_=acc[:], func=ACT.Copy, scale=gain_sb[:, blk, t : t + 1])
             nc.vector.tensor_tensor(
-                out=pages[i][:].indirect(half_list(idx2, c)), in0=h[:], in1=wgs_sb[c][:, t, :], op=MULT
+                out=pages[i][:].indirect(idx2[:, entries.start // 16 : entries.stop // 16]),
+                in0=h[:], in1=wgs_sb[c][:, t, cols], op=MULT,
             )
+
+        whole_half = slice(0, HALF)
 
         with tc.tile_pool(name="head", bufs=1) as head:
             tab_sb = [head.tile([P, T], I32, name=f"tab_sb{a}") for a in range(2)]
             tab_scales_sb = head.tile([P, T], U8)
             w1_raw = [head.tile([P, PACK, R], F32, name=f"w1_raw{a}") for a in range(2)]
-            w3_raw = [head.tile([P, 2, HALF], I32, name=f"w3_raw{b}") for b in range(2)]
+            w3_raw = [head.tile([P, 2, PASS], I32, name=f"w3_raw{b}") for b in range(2)]
             w2_raw = head.tile([P, 2 * H], U8)
             w23_scales_raw = head.tile([P, H], U8)
 
@@ -112,12 +123,12 @@ def tile_list_perfusion_console_page_kernel(
             def load_w3(blk):
                 w3_bytes = w3_words.rearrange("a p n i -> p a (n i)")
                 nc.sync.dma_start(
-                    out=w3_raw[blk][:], in_=w3_bytes[:, :, 4 * HALF * blk : 4 * HALF * (blk + 1)].bitcast(I32)
+                    out=w3_raw[blk][:], in_=w3_bytes[:, :, PACK * PASS * blk : PACK * PASS * (blk + 1)].bitcast(I32)
                 )
 
             def load_w1(a):
                 nc.sync.dma_start(
-                    out=w1_raw[a][:], in_=w1[512 * a : 512 * (a + 1), :].rearrange("(p j) m -> p j m", j=PACK)
+                    out=w1_raw[a][:], in_=w1[PASS * a : PASS * (a + 1), :].rearrange("(p j) m -> p j m", j=PACK)
                 )
 
             def load_tab(a):
@@ -151,14 +162,11 @@ def tile_list_perfusion_console_page_kernel(
             load_page(0)
             load_w3(1)
             load_page(1)
-            load_wgs(0, slice(2, 4))
-            for i in range(2, 8):
+            load_wgs(0, slice(2, PACK))
+            for i in range(2, ROW_TILES):
                 load_page(i)
-            load_wgs(1, slice(0, 4))
+            load_wgs(1, slice(0, PACK))
             nc.sync.dma_start(out=wean_sb[:], in_=wean.rearrange("(b p t) -> p b t", b=2, t=PACK))
-
-            warm = head.tile([P, 1], F32)
-            nc.scalar.activation(out=warm[:], in_=g1_sb[:, 0:1], func=ACT.Tanh)
 
             def deal_w3(blk):
                 nc.vector.tensor_copy(
@@ -198,6 +206,7 @@ def tile_list_perfusion_console_page_kernel(
                 out=w2_codes[:].bitcast(U16).rearrange("p (b t c i) -> p b c t i", b=2, t=PACK, i=8),
                 in_=w2_raw[:].bitcast(U16).rearrange("p (b c i t) -> p b c t i", b=2, t=PACK, i=8),
             )
+
             unit_cols = [slice(u * UNIT, (u + 1) * UNIT) for u in range(HALF // UNIT)]
             unit_acc = [bank(u, [P, PACK, UNIT]) for u in range(HALF // UNIT)]
             for u, cols in enumerate(unit_cols):
@@ -210,7 +219,10 @@ def tile_list_perfusion_console_page_kernel(
                 in_=w23_scales_raw[:].rearrange("p (b c i t) -> p b c t i", b=2, t=PACK, i=16),
             )
 
-            b_grouped = [pool.tile([P, HALF, PACK], BF16, name=f"b_grouped{c}", align_bytes=64) for c, pool in enumerate((keep, head))]
+            b_grouped = [
+                pool.tile([P, HALF, PACK], BF16, name=f"b_grouped{c}", align_bytes=64)
+                for c, pool in enumerate((keep, head))
+            ]
             for u, cols in enumerate(unit_cols):
                 for t in range(PACK):
                     features(unit_acc[u][:, t, :], t, 1, 0, cols, False, t == PACK - 1)
@@ -226,23 +238,23 @@ def tile_list_perfusion_console_page_kernel(
                         out=b_codes[0][:, pair].bitcast(E4M3), scales=b_scales[0][:, pair],
                         in_=b_grouped[0][:, pair, :].rearrange("p n t -> p (n t)"),
                     )
+            for q, h_name in enumerate(("h0", "h_spare")):
+                new_states(0, 0, bank(4 + q, [P, 2 * UNIT]), slice(2 * UNIT * q, 2 * UNIT * (q + 1)), h_name)
             gather_words(1, 1, "b_grouped0")
-
-            for i in range(8):
-                if i == 1:
-                    deal_w3(1)
-                new_states(i, 0, bank(4 + i if i < 2 else 6 + i % 2, [P, HALF]))
+            deal_w3(1)
+            for i in range(1, ROW_TILES):
+                new_states(i, 0, bank(6 + i % 2, [P, HALF]), whole_half, f"h{i}")
 
             for t in range(PACK):
                 acc = bank(4 + t % 2, [P, HALF])
                 for a in range(2):
-                    features(acc[:], t, a, 1, slice(0, HALF), a == 0, a == 1)
+                    features(acc[:], t, a, 1, whole_half, a == 0, a == 1)
                 bounded = head.tile([P, HALF], F32, name="bounded", bufs=2)
                 nc.scalar.activation(out=bounded[:], in_=acc[:], func=ACT.Tanh)
                 nc.scalar.activation(
                     out=b_grouped[1][:, :, t], in_=bounded[:], func=ACT.Copy, scale=g1_sb[:, t : t + 1]
                 )
-            b_codes.append(keep.tile([P, HALF], U32, name="h4", align_bytes=64))
+            b_codes.append(keep.tile([P, HALF], U32, name=f"h{B_LATE_TILE}", align_bytes=64))
             nc.vector.quantize_mx(
                 out=b_codes[1][:].bitcast(E4M3), scales=b_scales[1][:],
                 in_=b_grouped[1][:].rearrange("p n t -> p (n t)"),
@@ -255,8 +267,13 @@ def tile_list_perfusion_console_page_kernel(
         w4_scales = tail.tile([P, n_tiles, 2 * P], U8, align_bytes=64)
         wgo_sb = tail.tile([P, S], F32)
         pumps = [tail.tile([P, T2], F32, name=f"pump{n}") for n in range(n_tiles)]
-        x_grouped = [[tail.tile([P, HALF, PACK], BF16, name=f"x_grouped{b}{c}", align_bytes=64) for c in range(2)] for b in range(2)]
-        x_scales = [[tail.tile([P, HALF], U8, name=f"x_scales{b}{c}", align_bytes=64) for c in range(2)] for b in range(2)]
+        x_grouped = [
+            [tail.tile([P, HALF, PACK], BF16, name=f"x_grouped{b}{c}", align_bytes=64) for c in range(2)]
+            for b in range(2)
+        ]
+        x_scales = [
+            [tail.tile([P, HALF], U8, name=f"x_scales{b}{c}", align_bytes=64) for c in range(2)] for b in range(2)
+        ]
         y_acc = [[bank(3 * c + n, [P, HALF]) for n in range(n_tiles)] for c in range(2)]
 
         nc.sync.dma_start(out=w4_raw[:], in_=w4.rearrange("(b p j) n -> p b j n", b=2, j=PACK))
@@ -281,14 +298,13 @@ def tile_list_perfusion_console_page_kernel(
                     out=x_grouped[blk][c][:, :, t], in_=picked[:, k, :], func=ACT.Copy, scale=wean_sb[:, blk, t : t + 1]
                 )
 
-        new_states(0, 1, bank(6, [P, HALF]))
-        for i in range(1, 8):
-            new_states(i, 1, bank(6 + i % 2, [P, HALF]))
-            if i < 7:
+        for i in range(ROW_TILES):
+            new_states(i, 1, bank(6 + i % 2, [P, HALF]), whole_half, "h_spare" if i == B_LATE_TILE else f"h{i}")
+            if 0 < i < ROW_TILES - 1:
                 recall(i - 1, (0, 1))
         for c in range(2):
-            recall(6, (c,))
-            recall(7, (c,))
+            recall(ROW_TILES - 2, (c,))
+            recall(ROW_TILES - 1, (c,))
 
         late_codes = keep.tile([P, 2 * N + 2 * HALF], U32, name="wgs_sb1", align_bytes=64)
         w4_codes = [late_codes[:, 2 * P * n : 2 * P * (n + 1)] for n in range(n_tiles)]

from contextlib import ExitStack

import concourse.mybir as mybir

K, R, H, N, T, S, T2 = 1024, 512, 1024, 384, 4096, 1024, 2048
FLOPS = 2 * S * (K * R + R * H + K * H + H * N)

F32 = mybir.dt.float32
BF16 = mybir.dt.bfloat16
I32 = mybir.dt.int32
U32 = mybir.dt.uint32
U16 = mybir.dt.uint16
U8 = mybir.dt.uint8
E4M3 = mybir.dt.float8_e4m3fn_x4
E2M1 = mybir.dt.float4_e2m1fn_x4
ACT = mybir.ActivationFunctionType
MULT = mybir.AluOpType.mult

P = 128
PACK = 4
PASS = P * PACK
HALF = 512
UNIT = 128
LIST_COLS = HALF // 16
ROW_TILES = H // P
B_LATE_TILE = 4


def tile_list_perfusion_console_page_kernel(
    tc, tab_words, tab_scales, offs, offs2, offs3, offs4, w1, g1, w2_words, w2_scales,
    w3_words, w3_scales, gain, wgs, page0, wean, w4, wgo, page1, out,
):
    nc = tc.nc

    def half_cols(c):
        return slice(c * HALF, (c + 1) * HALF)

    def half_list(lst, c):
        return lst[:, c * LIST_COLS : (c + 1) * LIST_COLS]

    with ExitStack() as ctx:
        keep = ctx.enter_context(tc.tile_pool(name="keep", bufs=1))
        psum = ctx.enter_context(tc.psum_pool(name="psum", bufs=1))

        def bank(i, shape):
            return psum.tile(shape, F32, name=f"bank{i}")

        idx = keep.tile([P, S // 16], U16)
        idx2 = keep.tile([P, S // 16], U16)
        idx3 = keep.tile([P, S // 16], U16)
        idx4 = keep.tile([P, S // 16], U16)
        g1_sb = keep.tile([P, PACK], F32)
        gain_sb = keep.tile([P, 2, PACK], F32)
        wean_sb = keep.tile([P, 2, PACK], F32)
        v_codes = {}
        v_scales = keep.tile([P, S], U8, align_bytes=64)
        w1_codes = [keep.tile([P, R], U32, name=f"w1_codes{a}", align_bytes=64) for a in range(2)]
        w1_scales = [keep.tile([P, R], U8, name=f"w1_scales{a}", align_bytes=64) for a in range(2)]
        w3_codes = [keep.tile([P, 2, PASS], I32, name=f"w3_codes{b}", align_bytes=64) for b in range(2)]
        w2_codes = keep.tile([P, 2 * H], U8, align_bytes=64)
        w23_scales = keep.tile([P, H], U8, align_bytes=64)
        b_codes = [keep.tile([P, HALF], U32, name="b_codes0", align_bytes=64)]
        b_scales = [keep.tile([P, HALF], U8, name=f"b_scales{c}", align_bytes=64) for c in range(2)]
        wgs_sb = [keep.tile([P, PACK, HALF], F32, name=f"wgs_sb{c}", align_bytes=64) for c in range(2)]
        pages = [keep.tile([P, T2], F32, name=f"page{i}") for i in range(ROW_TILES)]

        def load_wgs(c, slots):
            rows = wgs.rearrange("(q t) s -> q t s", t=PACK)[:, slots, half_cols(c)]
            for quad in (0, 2, 1, 3):
                nc.sync.dma_start(out=wgs_sb[c][32 * quad : 32 * quad + 32, slots, :], in_=rows)

        def new_states(i, c, acc, cols, h_name):
            blk, t = divmod(i, PACK)
            dealt = slice(i * P, (i + 1) * P)
            width = cols.stop - cols.start
            entries = slice(c * HALF + cols.start, c * HALF + cols.stop)
            for a in range(2):
                nc.tensor.matmul_mx(
                    out=acc[:], lhsT=w3_codes[blk][:, a, t * P : (t + 1) * P].bitcast(E4M3),
                    lhsT_scale=w23_scales[4 + 4 * a : P, dealt],
                    rhs=v_codes[a, c][:, cols].bitcast(E4M3), rhs_scale=v_scales[4 * a : P, entries],
                    start=(a == 0), stop=False,
                )
            step = HALF if width == HALF else UNIT
            for lo in range(0, width, step):
                part = slice(cols.start + lo, cols.start + lo + step)
                nc.tensor.matmul_mx(
                    out=acc[:, lo : lo + step], lhsT=w2_codes[:, 2 * i * P : 2 * (i + 1) * P].bitcast(E2M1),
                    lhsT_scale=w23_scales[:, dealt],
                    rhs=b_codes[c][:, part].bitcast(E4M3), rhs_scale=b_scales[c][:, part],
                    start=False, stop=(lo + step == width),
                )
            h = keep.tile([P, width], F32, name=h_name, align_bytes=64)
            nc.scalar.activation(out=h[:], in_=acc[:], func=ACT.Copy, scale=gain_sb[:, blk, t : t + 1])
            nc.vector.tensor_tensor(
                out=pages[i][:].indirect(idx2[:, entries.start // 16 : entries.stop // 16]),
                in0=h[:], in1=wgs_sb[c][:, t, cols], op=MULT,
            )

        whole_half = slice(0, HALF)

        with tc.tile_pool(name="head", bufs=1) as head:
            tab_sb = [head.tile([P, T], I32, name=f"tab_sb{a}") for a in range(2)]
            tab_scales_sb = head.tile([P, T], U8)
            w1_raw = [head.tile([P, PACK, R], F32, name=f"w1_raw{a}") for a in range(2)]
            w3_raw = [head.tile([P, 2, PASS], I32, name=f"w3_raw{b}") for b in range(2)]
            w2_raw = head.tile([P, 2 * H], U8)
            w23_scales_raw = head.tile([P, H], U8)

            nc.gpsimd.memset(tab_scales_sb[:].bitcast(I32), 0)
            nc.gpsimd.memset(w23_scales_raw[:].bitcast(I32), 0)
            for quad in range(4):
                nc.gpsimd.dma_start(
                    out=tab_scales_sb[32 * quad : 32 * quad + 8, :].bitcast(I32),
                    in_=tab_scales[:, 4 * quad : 4 * quad + 4, :].bitcast(I32),
                )
            for quad in range(4):
                nc.gpsimd.dma_start(
                    out=w23_scales_raw[32 * quad + 4 : 32 * quad + 12, :].bitcast(I32),
                    in_=w3_scales[:, 4 * quad : 4 * quad + 4, :].bitcast(I32),
                )

            def load_w3(blk):
                w3_bytes = w3_words.rearrange("a p n i -> p a (n i)")
                nc.sync.dma_start(
                    out=w3_raw[blk][:], in_=w3_bytes[:, :, PACK * PASS * blk : PACK * PASS * (blk + 1)].bitcast(I32)
                )

            def load_w1(a):
                nc.sync.dma_start(
                    out=w1_raw[a][:], in_=w1[PASS * a : PASS * (a + 1), :].rearrange("(p j) m -> p j m", j=PACK)
                )

            def load_tab(a):
                nc.sync.dma_start(out=tab_sb[a][:], in_=tab_words[a].rearrange("p t i -> p (t i)").bitcast(I32))

            def load_page(i):
                rows = page0.rearrange("(b p t) c -> b t p c", b=2, t=PACK)
                nc.sync.dma_start(out=pages[i][:], in_=rows[i // PACK, i % PACK])

            def load_w2_scales(quad):
                nc.sync.dma_start(
                    out=w23_scales_raw[32 * quad : 32 * quad + 4, :].bitcast(I32),
                    in_=w2_scales[0, 4 * quad : 4 * quad + 4, :].bitcast(I32),
                )

            nc.sync.dma_start(idx[:], offs)
            load_tab(0)
            load_w1(0)
            nc.sync.dma_start(out=g1_sb[:], in_=g1.rearrange("(p t) -> p t", t=PACK))
            nc.sync.dma_start(out=gain_sb[:], in_=gain.rearrange("(b p t) -> p b t", b=2, t=PACK))
            nc.sync.dma_start(idx2[:], offs2)
            nc.sync.dma_start(idx3[:], offs3)
            nc.sync.dma_start(idx4[:], offs4)
            load_w1(1)
            nc.sync.dma_start(out=w2_raw[:].bitcast(I32), in_=w2_words[0].bitcast(I32))
            load_tab(1)
            load_w3(0)
            for quad in range(4):
                load_w2_scales(quad)
            load_wgs(0, slice(0, 2))
            load_page(0)
            load_w3(1)
            load_page(1)
            load_wgs(0, slice(2, PACK))
            for i in range(2, ROW_TILES):
                load_page(i)
            load_wgs(1, slice(0, PACK))
            nc.sync.dma_start(out=wean_sb[:], in_=wean.rearrange("(b p t) -> p b t", b=2, t=PACK))

            def deal_w3(blk):
                nc.vector.tensor_copy(
                    out=w3_codes[blk][:].rearrange("p a (t c i) -> p a c t i", t=PACK, i=4),
                    in_=w3_raw[blk][:].rearrange("p a (c i t) -> p a c t i", t=PACK, i=4),
                )

            def quantise_w1(a):
                grouped = head.tile([P, PACK * R], BF16, name=f"w1_grouped{a}", align_bytes=64)
                nc.scalar.copy(
                    out=grouped[:].rearrange("p (t m j) -> p m t j", t=PACK, j=PACK),
                    in_=w1_raw[a][:].rearrange("p j (m t) -> p m t j", t=PACK),
                )
                nc.vector.quantize_mx(out=w1_codes[a][:].bitcast(E4M3), scales=w1_scales[a][:], in_=grouped[:])

            def gather_words(a, c, name):
                v_codes[a, c] = keep.tile([P, HALF], U32, name=name, align_bytes=64)
                nc.vector.tensor_copy(
                    out=v_codes[a, c][:], in_=tab_sb[a][:].bitcast(U32).indirect(half_list(idx, c))
                )

            def features(acc, t, a, c, cols, start, stop):
                nc.tensor.matmul_mx(
                    out=acc, lhsT=w1_codes[a][:, t * P : (t + 1) * P].bitcast(E4M3),
                    lhsT_scale=w1_scales[a][:, t * P : (t + 1) * P],
                    rhs=v_codes[a, c][:, cols].bitcast(E4M3),
                    rhs_scale=v_scales[4 * a : P, c * HALF + cols.start : c * HALF + cols.stop],
                    start=start, stop=stop,
                )

            gather_words(0, 0, "v_codes00")
            gather_words(0, 1, "v_codes01")
            nc.vector.tensor_copy(out=v_scales[:], in_=tab_scales_sb[:].indirect(idx[:]))
            quantise_w1(0)
            quantise_w1(1)
            nc.vector.tensor_copy(
                out=w2_codes[:].bitcast(U16).rearrange("p (b t c i) -> p b c t i", b=2, t=PACK, i=8),
                in_=w2_raw[:].bitcast(U16).rearrange("p (b c i t) -> p b c t i", b=2, t=PACK, i=8),
            )

            unit_cols = [slice(u * UNIT, (u + 1) * UNIT) for u in range(HALF // UNIT)]
            unit_acc = [bank(u, [P, PACK, UNIT]) for u in range(HALF // UNIT)]
            for u, cols in enumerate(unit_cols):
                for t in range(PACK):
                    features(unit_acc[u][:, t, :], t, 0, 0, cols, t == 0, False)
            gather_words(1, 0, "v_codes10")
            deal_w3(0)
            nc.vector.tensor_copy(
                out=w23_scales[:].rearrange("p (b t c i) -> p b c t i", b=2, t=PACK, i=16),
                in_=w23_scales_raw[:].rearrange("p (b c i t) -> p b c t i", b=2, t=PACK, i=16),
            )

            b_grouped = [
                pool.tile([P, HALF, PACK], BF16, name=f"b_grouped{c}", align_bytes=64)
                for c, pool in enumerate((keep, head))
            ]
            for u, cols in enumerate(unit_cols):
                for t in range(PACK):
                    features(unit_acc[u][:, t, :], t, 1, 0, cols, False, t == PACK - 1)
                bounded = head.tile([P, UNIT, PACK], F32, name=f"bounded_unit{u}")
                nc.scalar.activation(out=bounded[:], in_=unit_acc[u][:].rearrange("p t n -> p n t"), func=ACT.Tanh)
                nc.vector.tensor_tensor(
                    out=b_grouped[0][:, cols, :], in0=bounded[:],
                    in1=g1_sb[:].unsqueeze(1).to_broadcast([P, UNIT, PACK]), op=MULT,
                )
                if u % 2 == 1:
                    pair = slice((u - 1) * UNIT, (u + 1) * UNIT)
                    nc.vector.quantize_mx(
                        out=b_codes[0][:, pair].bitcast(E4M3), scales=b_scales[0][:, pair],
                        in_=b_grouped[0][:, pair, :].rearrange("p n t -> p (n t)"),
                    )
            for q, h_name in enumerate(("h0", "h_spare")):
                new_states(0, 0, bank(4 + q, [P, 2 * UNIT]), slice(2 * UNIT * q, 2 * UNIT * (q + 1)), h_name)
            gather_words(1, 1, "b_grouped0")
            deal_w3(1)
            for i in range(1, ROW_TILES):
                new_states(i, 0, bank(6 + i % 2, [P, HALF]), whole_half, f"h{i}")

            for t in range(PACK):
                acc = bank(4 + t % 2, [P, HALF])
                for a in range(2):
                    features(acc[:], t, a, 1, whole_half, a == 0, a == 1)
                bounded = head.tile([P, HALF], F32, name="bounded", bufs=2)
                nc.scalar.activation(out=bounded[:], in_=acc[:], func=ACT.Tanh)
                nc.scalar.activation(
                    out=b_grouped[1][:, :, t], in_=bounded[:], func=ACT.Copy, scale=g1_sb[:, t : t + 1]
                )
            b_codes.append(keep.tile([P, HALF], U32, name=f"h{B_LATE_TILE}", align_bytes=64))
            nc.vector.quantize_mx(
                out=b_codes[1][:].bitcast(E4M3), scales=b_scales[1][:],
                in_=b_grouped[1][:].rearrange("p n t -> p (n t)"),
            )

        tail = ctx.enter_context(tc.tile_pool(name="tail", bufs=1))
        n_tiles = N // P
        w4_raw = tail.tile([P, 2, PACK, N], F32)
        w4_grouped = tail.tile([P, n_tiles, 2, P, PACK], BF16, align_bytes=64)
        w4_scales = tail.tile([P, n_tiles, 2 * P], U8, align_bytes=64)
        wgo_sb = tail.tile([P, S], F32)
        pumps = [tail.tile([P, T2], F32, name=f"pump{n}") for n in range(n_tiles)]
        x_grouped = [
            [tail.tile([P, HALF, PACK], BF16, name=f"x_grouped{b}{c}", align_bytes=64) for c in range(2)]
            for b in range(2)
        ]
        x_scales = [
            [tail.tile([P, HALF], U8, name=f"x_scales{b}{c}", align_bytes=64) for c in range(2)] for b in range(2)
        ]
        y_acc = [[bank(3 * c + n, [P, HALF]) for n in range(n_tiles)] for c in range(2)]

        nc.sync.dma_start(out=w4_raw[:], in_=w4.rearrange("(b p j) n -> p b j n", b=2, j=PACK))
        nc.sync.dma_start(out=wgo_sb[:], in_=wgo)
        for n in range(n_tiles):
            nc.sync.dma_start(out=pumps[n][:], in_=page1[n * P : (n + 1) * P, :])

        for n in range(n_tiles):
            for blk in range(2):
                nc.scalar.copy(
                    out=w4_grouped[:, n, blk].rearrange("p (c i) j -> p c j i", i=4),
                    in_=w4_raw[:, blk, :, n * P : (n + 1) * P].rearrange("p j (c i) -> p c j i", i=4),
                )

        def recall(i, halves):
            blk, t = divmod(i, PACK)
            picked = tail.tile([P, len(halves), HALF], F32, name="picked", bufs=4)
            entries = idx3[:, halves[0] * LIST_COLS : (halves[-1] + 1) * LIST_COLS]
            nc.vector.tensor_copy(out=picked[:].rearrange("p c n -> p (c n)"), in_=pages[i][:].indirect(entries))
            for k, c in enumerate(halves):
                nc.scalar.activation(
                    out=x_grouped[blk][c][:, :, t], in_=picked[:, k, :], func=ACT.Copy, scale=wean_sb[:, blk, t : t + 1]
                )

        for i in range(ROW_TILES):
            new_states(i, 1, bank(6 + i % 2, [P, HALF]), whole_half, "h_spare" if i == B_LATE_TILE else f"h{i}")
            if 0 < i < ROW_TILES - 1:
                recall(i - 1, (0, 1))
        for c in range(2):
            recall(ROW_TILES - 2, (c,))
            recall(ROW_TILES - 1, (c,))

        late_codes = keep.tile([P, 2 * N + 2 * HALF], U32, name="wgs_sb1", align_bytes=64)
        w4_codes = [late_codes[:, 2 * P * n : 2 * P * (n + 1)] for n in range(n_tiles)]
        x_codes = [
            [late_codes[:, 2 * N + c * HALF : 2 * N + (c + 1) * HALF] for c in range(2)],
            [tail.tile([P, HALF], U32, name=f"x_codes1{c}", align_bytes=64)[:] for c in range(2)],
        ]

        def quantise_w4(n):
            nc.vector.quantize_mx(
                out=w4_codes[n].bitcast(E4M3), scales=w4_scales[:, n, :],
                in_=w4_grouped[:, n].rearrange("p b m j -> p (b m j)"),
            )

        def quantise_x(blk, c):
            nc.vector.quantize_mx(
                out=x_codes[blk][c].bitcast(E4M3), scales=x_scales[blk][c][:],
                in_=x_grouped[blk][c][:].rearrange("p n t -> p (n t)"),
            )

        def pump_pass(n, blk, c):
            cols = slice(blk * P, (blk + 1) * P)
            nc.tensor.matmul_mx(
                out=y_acc[c][n][:], lhsT=w4_codes[n][:, cols].bitcast(E4M3), lhsT_scale=w4_scales[:, n, cols],
                rhs=x_codes[blk][c].bitcast(E4M3), rhs_scale=x_scales[blk][c][:],
                start=(blk == 0), stop=(blk == 1),
            )

        def place(n, c):
            y = tail.tile([P, HALF], F32, name=f"y{n}{c}")
            nc.scalar.activation(out=y[:], in_=y_acc[c][n][:], func=ACT.Abs)
            nc.vector.tensor_tensor(
                out=pumps[n][:].indirect(half_list(idx4, c)), in0=y[:], in1=wgo_sb[:, half_cols(c)], op=MULT
            )

        quantise_w4(0)
        quantise_x(0, 0)
        pump_pass(0, 0, 0)
        quantise_x(1, 0)
        pump_pass(0, 1, 0)
        for n in range(1, n_tiles):
            quantise_w4(n)
        quantise_x(0, 1)
        quantise_x(1, 1)
        place(0, 0)
        for n in range(1, n_tiles):
            for blk in range(2):
                pump_pass(n, blk, 0)
            place(n, 0)
        for n in range(n_tiles):
            for blk in range(2):
                pump_pass(n, blk, 1)
            place(n, 1)
            nc.sync.dma_start(out=out[n * P : (n + 1) * P, :], in_=pumps[n][:])
